import numpy as np, ml_dtypes
CORES = [9,10,11,14,17,18,19,22,49,50,51,54]
N = 12
import mx_ref
NC, K, S = 128, 2, 2
CNT = [[0,32,0,12,40,16,16,8,4,0,0,0],[0,0,8,24,4,4,16,0,20,16,36,0],[0,0,0,4,64,4,4,8,0,20,24,0],[20,0,36,0,0,4,8,0,24,36,0,0],[12,0,0,0,0,8,24,0,44,20,0,20],[52,8,0,0,4,0,4,24,4,0,24,8],[4,28,0,0,0,36,0,8,20,8,4,20],[4,24,4,24,4,0,0,0,0,4,4,60],[0,12,48,0,0,8,0,20,0,24,4,12],[8,4,8,52,4,16,20,0,4,0,8,4],[20,4,24,8,0,8,0,60,0,0,0,4],[8,16,0,4,8,24,36,0,8,0,24,0]]
OFF = [[sum(c[:f]) for f in range(N + 1)] for c in CNT]
BF = ml_dtypes.bfloat16
def setup_inputs(rng):
    def f(*shape):
        return mx_ref.flush((rng.standard_normal(shape, dtype=np.float32) * np.exp2(rng.integers(-2, 3, shape[:-1] + (1,)))).astype(BF))
    return {"w": f(N, 128, 512), "x": f(N, 128, 4 * NC)}
def setup_inputs_blocks(rng):
    d = setup_inputs(rng)
    for k in ("w", "x"): d[k] = mx_ref.spread(d[k], rng, 1)
    return d
def setup_inputs_wide(rng):
    d = setup_inputs(rng)
    for k in ("x",): d[k] = mx_ref.flush((d[k].astype(np.float32) * np.exp2(rng.integers(-8, 9, (N, 1, 1))).astype(np.float32)).astype(BF))
    return d
def setup_inputs_zeros(rng):
    d = setup_inputs(rng); v = d["x"].reshape(N, 128, -1, 4).copy()
    v[np.broadcast_to((rng.random((N, 1, v.shape[2], 1)) < 0.33), v.shape)] = 0
    d["x"] = v.reshape(d["x"].shape)
    return d
def reference(w, x):
    y = np.zeros((N, 128, NC), np.float32)
    for k in range(K):
        for e in range(N):
            f = (e - S * k) % N
            t = np.concatenate([x[j][:, 4 * OFF[j][f]:4 * OFF[j][f + 1]] for j in range(N)], axis=1)
            p = mx_ref.matmul(mx_ref.quantize(w[e]), mx_ref.quantize(t)); c = 0
            for j in range(N):
                a, b = OFF[j][f], OFF[j][f + 1]
                y[j][:, a:b] = p[:, c:c + b - a] if k == 0 else y[j][:, a:b] + p[:, c:c + b - a]; c += b - a
    return {"y": y}

from concourse.bass import DstId, RemoteDMATransfer
from concourse.mybir import dt, AluOpType

N = 12
TW = 128
BANK = 512
NBANK = 8

SCRATCH = {
    "wb": ("sbuf", [128, 4 * TW], "bfloat16"),
    "xb": ("sbuf", [128, 4 * TW], "bfloat16"),
    "wq": ("sbuf", [128, N * TW], "float8_e4m3fn_x4"),
    "ws": ("sbuf", [128, N * TW], "uint8"),
    "xq": ("sbuf", [128, TW], "float8_e4m3fn_x4"),
    "xs": ("sbuf", [128, TW], "uint8"),
    "ps": ("psum", [128, NBANK * BANK], "float32"),
    "ysb": ("sbuf", [128, TW], "float32"),
}
SEMAPHORES = (["ldw", "ldx", "qw", "qx", "mm", "vs", "st", "snt"]
              + ["c%d" % e for e in range(N)] + ["s%d" % e for e in range(N)])

KINDS = ("s", "c")


def _bits(m):
    return [i for i in range(m.bit_length()) if (m >> i) & 1]


def _pow2(n):
    p = 1
    while 2 * p <= n:
        p *= 2
    return p


def make_plan(cores, cnt, topo):
    n = len(cores)
    need = [[cnt[j][e] > 0 or cnt[j][(e - 2) % n] > 0 for e in range(n)] for j in range(n)]
    chip = [topo.chip(c) for c in cores]
    chips = sorted(set(chip))
    on_chip = {ch: [r for r in range(n) if chip[r] == ch] for ch in chips}
    free = [all(topo.may_write(cores[r], d) for d in cores if d != cores[r]) for r in range(n)]

    sender = {}
    for ch in chips:
        load = {}
        for r in on_chip[ch]:
            if free[r]:
                sender[r] = r
                load[topo.die(cores[r])] = load.get(topo.die(cores[r]), 0) + 1
        for e in on_chip[ch]:
            if not free[e]:
                cand = [r for r in on_chip[ch] if free[r] and need[r][e]]
                r = min(cand, key=lambda q: (load[topo.die(cores[q])], q))
                sender[e] = r
                load[topo.die(cores[r])] += 1
    late = [sender[e] != e for e in range(n)]

    slot, bundles = {}, {}
    for ch in chips:
        order, bundles[ch] = [], []
        for src in chips:
            if src == ch:
                continue
            for b in [[e for e in on_chip[src] if not late[e]]] + [[e] for e in on_chip[src] if late[e]]:
                bundles[ch].append(b)
                order += b
        order += on_chip[ch]
        slot[ch] = {e: i for i, e in enumerate(order)}

    gate = {}
    for ch in chips:
        load = {r: sum(1 for e in range(n) if sender[e] == r) for r in on_chip[ch]}
        for b in sorted(bundles[ch], key=lambda b: (late[b[0]], -len(b), sum(need[q][b[0]] for q in on_chip[ch]), b[0])):
            r = min(on_chip[ch], key=lambda q: (load[q], -sum(need[q][e] for e in b), q))
            load[r] += 10
            for e in b:
                gate[(ch, e)] = r

    jobs = {r: [] for r in range(n)}
    arr, cls = {}, {}

    def job(src, tiles, kind, waits, groups):
        groups = [(engs, dests) for engs, dests in groups if dests]
        if not groups:
            return
        for engs, dests in groups:
            for d in dests:
                for e in tiles:
                    arr[(d, kind, e)] = (kind + str(tiles[0]), len(engs))
        jobs[src].append((waits, kind, tiles, groups))

    def engines(r):
        peer = [c for c in cores if c != cores[r] and topo.chip(c) == chip[r]][0]
        far = [c for c in cores if topo.chip(c) != chip[r]][0]
        allof = _bits(topo.mask(cores[r], peer))
        off = [b for b in allof if b in _bits(topo.mask(cores[r], far))]
        return allof, off, [b for b in allof if b not in off]

    def off_chip(src, e, own):
        _, off, _ = engines(src)
        dst = [ch for ch in chips if ch != chip[e]]
        per = _pow2(len(off) // len(dst))
        for kind in KINDS:
            waits = [("qw", 1)] if own else [arr[(src, kind, e)]]
            job(src, [e], kind, waits, [(off[i * per:(i + 1) * per], [gate[(ch, e)]]) for i, ch in enumerate(dst)])

    for e in range(n):
        if not late[e]:
            off_chip(e, e, True)
        else:
            _, off, _ = engines(e)
            for kind in KINDS:
                job(e, [e], kind, [("qw", 1)], [(off, [sender[e]])])
    for e in range(n):
        if late[e]:
            off_chip(sender[e], e, False)
    for e in range(n):
        _, _, rest = engines(e)
        peers = [r for r in on_chip[chip[e]] if r != e and need[r][e] and r != sender[e]]
        for kind in KINDS:
            job(e, [e], kind, [("qw", 1)], [(rest, peers)])
        for r in on_chip[chip[e]]:
            cls[(r, e)] = 0
    for ch in chips:
        for b in bundles[ch]:
            r = gate[(ch, b[0])]
            allof, _, _ = engines(r)
            dests = [q for q in on_chip[ch] if q != r and any(need[q][e] for e in b)]
            for kind in KINDS:
                job(r, b, kind, [arr[(r, kind, e)] for e in b], [(allof, dests)])
            for e in b:
                cls[(r, e)] = 3 if late[e] else 1
                for q in dests:
                    cls[(q, e)] = 4 if late[e] else 2
    return need, jobs, arr, cls, slot


def rank_program(g, core, T, topo):
    rank = T.rank_of(core)
    if rank is None:
        return
    cores = list(T.cores)
    cnt = T.tables["CNT"]
    need, jobs, arr, cls, slot = make_plan(cores, cnt, topo)
    S = T.sem

    def cols(c, tiles):
        sl = slot[topo.chip(c)]
        return slice(sl[tiles[0]] * TW, (sl[tiles[-1]] + 1) * TW)

    def view(kind, c, tiles):
        return T.wq[:, cols(c, tiles)].bitcast(dt.uint8) if kind == "c" else T.ws[:, cols(c, tiles)]

    g.sync.dma_start(T.wb[:], T.w[:]).then_inc(S.ldw, 16)
    g.sync.dma_start(T.xb[:], T.x[:]).then_inc(S.ldx, 16)
    g.vector.wait_ge(S.ldw, 16)
    g.vector.quantize_mx(T.wq[:, cols(core, [rank])], T.ws[:, cols(core, [rank])], T.wb[:]).then_inc(S.qw, 1)
    g.vector.wait_ge(S.ldx, 16)
    g.vector.quantize_mx(T.xq[:], T.xs[:], T.xb[:]).then_inc(S.qx, 1)

    sent = 0
    for waits, kind, tiles, groups in jobs[rank]:
        for name, val in waits:
            g.wait_ge(S[name], val)
        trs = []
        for engs, dests in groups:
            ids = []
            for d in dests:
                rid, pid, _ = topo.addr(cores[d])
                ids.append(DstId(rid=rid, pnc=pid))
            trs.append(RemoteDMATransfer(dst_ids=ids, dma_engine_mask=sum(1 << b for b in engs),
                                         remote_sem=S[kind + str(tiles[0])], srcs=[view(kind, core, tiles)],
                                         dsts=[view(kind, cores[d], tiles) for d in dests]))
            sent += len(engs)
        g.remote_dma_fused(trs, local_sem=S.snt)

    off = [sum(cnt[rank][:f]) for f in range(N + 1)]
    order = sorted([e for e in range(N) if need[rank][e]], key=lambda e: (cls[(rank, e)], e))
    first = {}
    nv = 0
    after = []
    g.tensor.wait_ge(S.qx, 1)
    for k, e in enumerate(order):
        base = (k % NBANK) * BANK
        for kind in KINDS:
            g.tensor.wait_ge(S[arr[(rank, kind, e)][0]], arr[(rank, kind, e)][1])
        if k >= NBANK:
            g.tensor.wait_ge(S.vs, after[k - NBANK])
        g.tensor.matmul_mx(T.ps[:, base:base + TW], T.wq[:, cols(core, [e])], T.ws[:, cols(core, [e])],
                           T.xq[:], T.xs[:], True, True).then_inc(S.mm, 1)
        g.vector.wait_ge(S.mm, k + 1)
        for f in (e, (e - 2) % N):
            a, b = off[f], off[f + 1]
            if a == b:
                continue
            if f not in first:
                g.vector.tensor_copy(T.ysb[:, a:b], T.ps[:, base + a:base + b]).then_inc(S.vs, 1)
                nv += 1
                first[f] = nv
            else:
                g.vector.wait_ge(S.vs, first[f])
                g.vector.tensor_tensor(T.ysb[:, a:b], T.ysb[:, a:b], T.ps[:, base + a:base + b],
                                       AluOpType.add).then_inc(S.vs, 1)
                nv += 1
        after.append(nv)

    g.sync.wait_ge(S.vs, nv)
    g.sync.dma_start(T.y[:], T.ysb[:]).then_inc(S.st, 16)
    g.sync.wait_ge(S.st, 16)
    g.wait_ge(S.snt, sent)
